import numpy as np, ml_dtypes
CORES = [6,22,38,54,70,86,102,118,134,150,166,182,198,214,230,246]
N = 16
def setup_inputs(rng):
    return {"x": rng.standard_normal((N, 128, 4096), dtype=np.float32).astype(ml_dtypes.bfloat16)}
def reference(x):
    s = x.sum(axis=0, dtype=np.float64).astype(x.dtype)
    return {"y": np.broadcast_to(s, (N,) + s.shape)}

@@ -1,0 +1,69 @@
+from concourse.bass import DstId, RemoteDMATransfer
+R = 16
+CHUNKS = [(68, None, 0, 0), (68, None, 0, 1), (66, None, 0, 2), (54, None, 0, 3)]
+ORDER = list(range(len(CHUNKS)))
+MAXC = 12
+SCRATCH = {}
+for k in range(MAXC):
+    shape = [R, 128, CHUNKS[k][0]] if k < len(CHUNKS) else [1, 128, 2]
+    SCRATCH['xs%d' % k] = ('dram', shape, 'bfloat16')
+    SCRATCH['ln%d' % k] = ('dram', shape, 'bfloat16')
+SEMAPHORES = ['ld%d' % k for k in range(MAXC)] + ['hp%d' % k for k in range(MAXC)] + ['rs%d' % k for k in range(MAXC)] + ['ag%d' % k for k in range(MAXC)] + ['sent', 'st']
+
+def rank_program(g, core, T, topo):
+    xs = [T.xs0, T.xs1, T.xs2, T.xs3, T.xs4, T.xs5, T.xs6, T.xs7, T.xs8, T.xs9, T.xs10, T.xs11]
+    ln = [T.ln0, T.ln1, T.ln2, T.ln3, T.ln4, T.ln5, T.ln6, T.ln7, T.ln8, T.ln9, T.ln10, T.ln11]
+    s = T.sem
+    ld = [s.ld0, s.ld1, s.ld2, s.ld3, s.ld4, s.ld5, s.ld6, s.ld7, s.ld8, s.ld9, s.ld10, s.ld11]
+    hp = [s.hp0, s.hp1, s.hp2, s.hp3, s.hp4, s.hp5, s.hp6, s.hp7, s.hp8, s.hp9, s.hp10, s.hp11]
+    rs = [s.rs0, s.rs1, s.rs2, s.rs3, s.rs4, s.rs5, s.rs6, s.rs7, s.rs8, s.rs9, s.rs10, s.rs11]
+    ag = [s.ag0, s.ag1, s.ag2, s.ag3, s.ag4, s.ag5, s.ag6, s.ag7, s.ag8, s.ag9, s.ag10, s.ag11]
+    pair, within = (core // 16, core % 16)
+    par, idx = (within // 8, within % 8)
+    base = pair * 16
+    row0 = [sum((c[0] for c in CHUNKS[:k])) // 2 for k in range(len(CHUNKS) + 1)]
+
+    def dst(d):
+        rid, pid = topo.addr(d, core)
+        return DstId(rid=rid, pnc=pid)
+
+    def scatter(k):
+        n, via, rpar, rcore = CHUNKS[k]
+        for half in range(2):
+            tr = []
+            for e in range(8):
+                j = (pair + half * 8 + e) % R
+                tr.append(RemoteDMATransfer(dst_ids=[dst(j * 16 + rpar * 8 + rcore)], dma_engine_mask=1 << e, remote_sem=rs[k], src=xs[k][j], dst=ln[k][pair]))
+            g.remote_dma_fused(tr, local_sem=s.sent)
+        return 16
+    sent = 0
+    if par == 0 and idx == 6:
+        for k in ORDER:
+            g.dma_start(xs[k][:], T.x[row0[k]:row0[k + 1], :]).then_inc(ld[k], 16)
+        for k in ORDER:
+            n, via, rpar, rcore = CHUNKS[k]
+            g.wait_ge(ld[k], 16)
+            if via is None:
+                sent += scatter(k)
+            else:
+                tr = [RemoteDMATransfer(dst_ids=[dst(base + via)], dma_engine_mask=1 << j, remote_sem=hp[k], src=xs[k][j], dst=xs[k][j]) for j in range(R)]
+                g.remote_dma_fused(tr, local_sem=s.sent)
+                sent += 16
+        for k in ORDER:
+            g.wait_ge(ag[k], 8 * R)
+            g.dma_start(T.y[row0[k]:row0[k + 1], :], ln[k][:]).then_inc(s.st, 16)
+        g.wait_ge(s.st, 16 * len(ORDER))
+        g.wait_ge(s.sent, sent)
+        return
+    for k in ORDER:
+        n, via, rpar, rcore = CHUNKS[k]
+        if par == 0 and via == idx:
+            g.wait_ge(hp[k], 16)
+            sent += scatter(k)
+        if par == rpar and idx == rcore:
+            g.wait_ge(rs[k], 16)
+            to = [(pair + t) % R for t in range(R)]
+            g.remote_dma_fused([RemoteDMATransfer(dst_ids=[dst(i * 16 + 6) for i in to], dma_engine_mask=255, remote_sem=ag[k], srcs=[ln[k][r] for r in range(R)], dsts=[ln[k][pair] for i in to], alu_op=1)], local_sem=s.sent)
+            sent += 8
+    if sent:
+        g.wait_ge(s.sent, sent)

@@ -1,27 +1,30 @@
 from concourse.bass import DstId, RemoteDMATransfer
+
 R = 16
 CHUNKS = [(68, None, 0, 0), (68, None, 0, 1), (66, None, 0, 2), (54, None, 0, 3)]
-ORDER = list(range(len(CHUNKS)))
-MAXC = 12
+NK = len(CHUNKS)
+MAXC = 8
 SCRATCH = {}
 for k in range(MAXC):
-    shape = [R, 128, CHUNKS[k][0]] if k < len(CHUNKS) else [1, 128, 2]
+    shape = [R, 128, CHUNKS[k][0]] if k < NK else [1, 128, 2]
     SCRATCH['xs%d' % k] = ('dram', shape, 'bfloat16')
     SCRATCH['ln%d' % k] = ('dram', shape, 'bfloat16')
-SEMAPHORES = ['ld%d' % k for k in range(MAXC)] + ['hp%d' % k for k in range(MAXC)] + ['rs%d' % k for k in range(MAXC)] + ['ag%d' % k for k in range(MAXC)] + ['sent', 'st']
+SEMAPHORES = (['ld%d' % k for k in range(MAXC)] + ['hp%d' % k for k in range(MAXC)] + ['rs%d' % k for k in range(MAXC)]
+              + ['ag%d' % k for k in range(MAXC)] + ['sent', 'st0', 'st1'])
+
 
 def rank_program(g, core, T, topo):
-    xs = [T.xs0, T.xs1, T.xs2, T.xs3, T.xs4, T.xs5, T.xs6, T.xs7, T.xs8, T.xs9, T.xs10, T.xs11]
-    ln = [T.ln0, T.ln1, T.ln2, T.ln3, T.ln4, T.ln5, T.ln6, T.ln7, T.ln8, T.ln9, T.ln10, T.ln11]
+    xs = [T.xs0, T.xs1, T.xs2, T.xs3, T.xs4, T.xs5, T.xs6, T.xs7]
+    ln = [T.ln0, T.ln1, T.ln2, T.ln3, T.ln4, T.ln5, T.ln6, T.ln7]
     s = T.sem
-    ld = [s.ld0, s.ld1, s.ld2, s.ld3, s.ld4, s.ld5, s.ld6, s.ld7, s.ld8, s.ld9, s.ld10, s.ld11]
-    hp = [s.hp0, s.hp1, s.hp2, s.hp3, s.hp4, s.hp5, s.hp6, s.hp7, s.hp8, s.hp9, s.hp10, s.hp11]
-    rs = [s.rs0, s.rs1, s.rs2, s.rs3, s.rs4, s.rs5, s.rs6, s.rs7, s.rs8, s.rs9, s.rs10, s.rs11]
-    ag = [s.ag0, s.ag1, s.ag2, s.ag3, s.ag4, s.ag5, s.ag6, s.ag7, s.ag8, s.ag9, s.ag10, s.ag11]
+    ld = [s.ld0, s.ld1, s.ld2, s.ld3, s.ld4, s.ld5, s.ld6, s.ld7]
+    hp = [s.hp0, s.hp1, s.hp2, s.hp3, s.hp4, s.hp5, s.hp6, s.hp7]
+    rs = [s.rs0, s.rs1, s.rs2, s.rs3, s.rs4, s.rs5, s.rs6, s.rs7]
+    ag = [s.ag0, s.ag1, s.ag2, s.ag3, s.ag4, s.ag5, s.ag6, s.ag7]
     pair, within = (core // 16, core % 16)
     par, idx = (within // 8, within % 8)
     base = pair * 16
-    row0 = [sum((c[0] for c in CHUNKS[:k])) // 2 for k in range(len(CHUNKS) + 1)]
+    row0 = [sum(c[0] for c in CHUNKS[:k]) // 2 for k in range(NK + 1)]
 
     def dst(d):
         rid, pid = topo.addr(d, core)
@@ -33,29 +36,38 @@ def rank_program(g, core, T, topo):
             tr = []
             for e in range(8):
                 j = (pair + half * 8 + e) % R
-                tr.append(RemoteDMATransfer(dst_ids=[dst(j * 16 + rpar * 8 + rcore)], dma_engine_mask=1 << e, remote_sem=rs[k], src=xs[k][j], dst=ln[k][pair]))
+                tr.append(RemoteDMATransfer(dst_ids=[dst(j * 16 + rpar * 8 + rcore)], dma_engine_mask=1 << e,
+                                            remote_sem=rs[k], src=xs[k][j], dst=ln[k][pair]))
             g.remote_dma_fused(tr, local_sem=s.sent)
         return 16
+
     sent = 0
     if par == 0 and idx == 6:
-        for k in ORDER:
-            g.dma_start(xs[k][:], T.x[row0[k]:row0[k + 1], :]).then_inc(ld[k], 16)
-        for k in ORDER:
+        q = [g.sync, g.scalar]
+        stq = [s.st0, s.st1]
+        for k in range(NK):
+            q[k % 2].dma_start(xs[k][:], T.x[row0[k]:row0[k + 1], :]).then_inc(ld[k], 16)
+        for k in range(NK):
             n, via, rpar, rcore = CHUNKS[k]
             g.wait_ge(ld[k], 16)
             if via is None:
                 sent += scatter(k)
             else:
-                tr = [RemoteDMATransfer(dst_ids=[dst(base + via)], dma_engine_mask=1 << j, remote_sem=hp[k], src=xs[k][j], dst=xs[k][j]) for j in range(R)]
+                tr = [RemoteDMATransfer(dst_ids=[dst(base + via)], dma_engine_mask=1 << j, remote_sem=hp[k],
+                                        src=xs[k][j], dst=xs[k][j]) for j in range(R)]
                 g.remote_dma_fused(tr, local_sem=s.sent)
                 sent += 16
-        for k in ORDER:
-            g.wait_ge(ag[k], 8 * R)
-            g.dma_start(T.y[row0[k]:row0[k + 1], :], ln[k][:]).then_inc(s.st, 16)
-        g.wait_ge(s.st, 16 * len(ORDER))
+        cnt = [0, 0]
+        for k in range(NK):
+            q[k % 2].wait_ge(ag[k], 8 * R)
+            q[k % 2].dma_start(T.y[row0[k]:row0[k + 1], :], ln[k][:]).then_inc(stq[k % 2], 16)
+            cnt[k % 2] += 16
+        for i in range(2):
+            if cnt[i]:
+                q[i].wait_ge(stq[i], cnt[i])
         g.wait_ge(s.sent, sent)
         return
-    for k in ORDER:
+    for k in range(NK):
         n, via, rpar, rcore = CHUNKS[k]
         if par == 0 and via == idx:
             g.wait_ge(hp[k], 16)
@@ -63,7 +75,9 @@ def rank_program(g, core, T, topo):
         if par == rpar and idx == rcore:
             g.wait_ge(rs[k], 16)
             to = [(pair + t) % R for t in range(R)]
-            g.remote_dma_fused([RemoteDMATransfer(dst_ids=[dst(i * 16 + 6) for i in to], dma_engine_mask=255, remote_sem=ag[k], srcs=[ln[k][r] for r in range(R)], dsts=[ln[k][pair] for i in to], alu_op=1)], local_sem=s.sent)
+            g.remote_dma_fused([RemoteDMATransfer(dst_ids=[dst(i * 16 + 6) for i in to], dma_engine_mask=255,
+                                                  remote_sem=ag[k], srcs=[ln[k][r] for r in range(R)],
+                                                  dsts=[ln[k][pair] for i in to], alu_op=1)], local_sem=s.sent)
             sent += 8
     if sent:
         g.wait_ge(s.sent, sent)

@@ -1,9 +1,10 @@
 from concourse.bass import DstId, RemoteDMATransfer
 
 R = 16
-CHUNKS = [(68, None, 0, 0), (68, None, 0, 1), (66, None, 0, 2), (54, None, 0, 3)]
+CHUNKS = [(32, 0, 0, 2), (32, None, 0, 4), (32, 1, 0, 3), (32, None, 0, 5), (32, 0, 0, 2), (32, None, 0, 7),
+          (20, 1, 0, 3), (28, None, 0, 4), (16, None, 0, 5)]
 NK = len(CHUNKS)
-MAXC = 8
+MAXC = 12
 SCRATCH = {}
 for k in range(MAXC):
     shape = [R, 128, CHUNKS[k][0]] if k < NK else [1, 128, 2]
@@ -14,13 +15,13 @@ SEMAPHORES = (['ld%d' % k for k in range(MAXC)] + ['hp%d' % k for k in range(MAX
 
 
 def rank_program(g, core, T, topo):
-    xs = [T.xs0, T.xs1, T.xs2, T.xs3, T.xs4, T.xs5, T.xs6, T.xs7]
-    ln = [T.ln0, T.ln1, T.ln2, T.ln3, T.ln4, T.ln5, T.ln6, T.ln7]
+    xs = [T.xs0, T.xs1, T.xs2, T.xs3, T.xs4, T.xs5, T.xs6, T.xs7, T.xs8, T.xs9, T.xs10, T.xs11]
+    ln = [T.ln0, T.ln1, T.ln2, T.ln3, T.ln4, T.ln5, T.ln6, T.ln7, T.ln8, T.ln9, T.ln10, T.ln11]
     s = T.sem
-    ld = [s.ld0, s.ld1, s.ld2, s.ld3, s.ld4, s.ld5, s.ld6, s.ld7]
-    hp = [s.hp0, s.hp1, s.hp2, s.hp3, s.hp4, s.hp5, s.hp6, s.hp7]
-    rs = [s.rs0, s.rs1, s.rs2, s.rs3, s.rs4, s.rs5, s.rs6, s.rs7]
-    ag = [s.ag0, s.ag1, s.ag2, s.ag3, s.ag4, s.ag5, s.ag6, s.ag7]
+    ld = [s.ld0, s.ld1, s.ld2, s.ld3, s.ld4, s.ld5, s.ld6, s.ld7, s.ld8, s.ld9, s.ld10, s.ld11]
+    hp = [s.hp0, s.hp1, s.hp2, s.hp3, s.hp4, s.hp5, s.hp6, s.hp7, s.hp8, s.hp9, s.hp10, s.hp11]
+    rs = [s.rs0, s.rs1, s.rs2, s.rs3, s.rs4, s.rs5, s.rs6, s.rs7, s.rs8, s.rs9, s.rs10, s.rs11]
+    ag = [s.ag0, s.ag1, s.ag2, s.ag3, s.ag4, s.ag5, s.ag6, s.ag7, s.ag8, s.ag9, s.ag10, s.ag11]
     pair, within = (core // 16, core % 16)
     par, idx = (within // 8, within % 8)
     base = pair * 16
@@ -43,25 +44,27 @@ def rank_program(g, core, T, topo):
 
     sent = 0
     if par == 0 and idx == 6:
-        q = [g.sync, g.scalar]
         stq = [s.st0, s.st1]
+        qi = [0 if c[1] is None else 1 for c in CHUNKS]
+        q = [g.sync, g.scalar]
         for k in range(NK):
-            q[k % 2].dma_start(xs[k][:], T.x[row0[k]:row0[k + 1], :]).then_inc(ld[k], 16)
+            q[qi[k]].dma_start(xs[k][:], T.x[row0[k]:row0[k + 1], :]).then_inc(ld[k], 16)
         for k in range(NK):
             n, via, rpar, rcore = CHUNKS[k]
             g.wait_ge(ld[k], 16)
             if via is None:
                 sent += scatter(k)
             else:
-                tr = [RemoteDMATransfer(dst_ids=[dst(base + via)], dma_engine_mask=1 << j, remote_sem=hp[k],
-                                        src=xs[k][j], dst=xs[k][j]) for j in range(R)]
-                g.remote_dma_fused(tr, local_sem=s.sent)
+                for half in range(2):
+                    tr = [RemoteDMATransfer(dst_ids=[dst(base + via)], dma_engine_mask=1 << (8 + e), remote_sem=hp[k],
+                                            src=xs[k][half * 8 + e], dst=xs[k][half * 8 + e]) for e in range(8)]
+                    g.remote_dma_fused(tr, local_sem=s.sent)
                 sent += 16
         cnt = [0, 0]
         for k in range(NK):
-            q[k % 2].wait_ge(ag[k], 8 * R)
-            q[k % 2].dma_start(T.y[row0[k]:row0[k + 1], :], ln[k][:]).then_inc(stq[k % 2], 16)
-            cnt[k % 2] += 16
+            q[qi[k]].wait_ge(ag[k], 8 * R)
+            q[qi[k]].dma_start(T.y[row0[k]:row0[k + 1], :], ln[k][:]).then_inc(stq[qi[k]], 16)
+            cnt[qi[k]] += 16
         for i in range(2):
             if cnt[i]:
                 q[i].wait_ge(stq[i], cnt[i])

@@ -1,8 +1,9 @@
 from concourse.bass import DstId, RemoteDMATransfer
 
 R = 16
-CHUNKS = [(32, 0, 0, 2), (32, None, 0, 4), (32, 1, 0, 3), (32, None, 0, 5), (32, 0, 0, 2), (32, None, 0, 7),
-          (20, 1, 0, 3), (28, None, 0, 4), (16, None, 0, 5)]
+CHUNKS = [(36, 0, 0, 2), (36, None, 0, 4), (34, 1, 0, 3), (34, None, 0, 5), (30, 0, 0, 1), (30, None, 0, 7),
+          (20, 1, 0, 0), (20, None, 0, 4), (16, None, 0, 5)]
+GROUPS = [(1, 0), (3, 2), (5, 4), (7, 6), (8, None)]
 NK = len(CHUNKS)
 MAXC = 12
 SCRATCH = {}
@@ -31,16 +32,19 @@ def rank_program(g, core, T, topo):
         rid, pid = topo.addr(d, core)
         return DstId(rid=rid, pnc=pid)
 
-    def scatter(k):
+    def direct(k, half):
         n, via, rpar, rcore = CHUNKS[k]
-        for half in range(2):
-            tr = []
-            for e in range(8):
-                j = (pair + half * 8 + e) % R
-                tr.append(RemoteDMATransfer(dst_ids=[dst(j * 16 + rpar * 8 + rcore)], dma_engine_mask=1 << e,
-                                            remote_sem=rs[k], src=xs[k][j], dst=ln[k][pair]))
-            g.remote_dma_fused(tr, local_sem=s.sent)
-        return 16
+        tr = []
+        for e in range(8):
+            j = (pair + half * 8 + e) % R
+            tr.append(RemoteDMATransfer(dst_ids=[dst(j * 16 + rpar * 8 + rcore)], dma_engine_mask=1 << e,
+                                        remote_sem=rs[k], src=xs[k][j], dst=ln[k][pair]))
+        return tr
+
+    def handover(k, half):
+        via = CHUNKS[k][1]
+        return [RemoteDMATransfer(dst_ids=[dst(base + via)], dma_engine_mask=1 << (8 + e), remote_sem=hp[k],
+                                  src=xs[k][half * 8 + e], dst=xs[k][half * 8 + e]) for e in range(8)]
 
     sent = 0
     if par == 0 and idx == 6:
@@ -49,17 +53,19 @@ def rank_program(g, core, T, topo):
         q = [g.sync, g.scalar]
         for k in range(NK):
             q[qi[k]].dma_start(xs[k][:], T.x[row0[k]:row0[k + 1], :]).then_inc(ld[k], 16)
-        for k in range(NK):
-            n, via, rpar, rcore = CHUNKS[k]
-            g.wait_ge(ld[k], 16)
-            if via is None:
-                sent += scatter(k)
-            else:
-                for half in range(2):
-                    tr = [RemoteDMATransfer(dst_ids=[dst(base + via)], dma_engine_mask=1 << (8 + e), remote_sem=hp[k],
-                                            src=xs[k][half * 8 + e], dst=xs[k][half * 8 + e]) for e in range(8)]
-                    g.remote_dma_fused(tr, local_sem=s.sent)
-                sent += 16
+        for kd, kr in GROUPS:
+            if kr is not None:
+                g.wait_ge(ld[kr], 16)
+            if kd is not None:
+                g.wait_ge(ld[kd], 16)
+            for half in range(2):
+                tr = []
+                if kd is not None:
+                    tr += direct(kd, half)
+                if kr is not None:
+                    tr += handover(kr, half)
+                g.remote_dma_fused(tr, local_sem=s.sent)
+                sent += len(tr)
         cnt = [0, 0]
         for k in range(NK):
             q[qi[k]].wait_ge(ag[k], 8 * R)
@@ -71,10 +77,13 @@ def rank_program(g, core, T, topo):
         g.wait_ge(s.sent, sent)
         return
     for k in range(NK):
-        n, via, rpar, rcore = CHUNKS[k]
-        if par == 0 and via == idx:
+        if par == 0 and CHUNKS[k][1] == idx:
             g.wait_ge(hp[k], 16)
-            sent += scatter(k)
+            for half in range(2):
+                g.remote_dma_fused(direct(k, half), local_sem=s.sent)
+            sent += 16
+    for k in range(NK):
+        n, via, rpar, rcore = CHUNKS[k]
         if par == rpar and idx == rcore:
             g.wait_ge(rs[k], 16)
             to = [(pair + t) % R for t in range(R)]

@@ -1,9 +1,9 @@
 from concourse.bass import DstId, RemoteDMATransfer
 
 R = 16
-CHUNKS = [(36, 0, 0, 2), (36, None, 0, 4), (34, 1, 0, 3), (34, None, 0, 5), (30, 0, 0, 1), (30, None, 0, 7),
-          (20, 1, 0, 0), (20, None, 0, 4), (16, None, 0, 5)]
-GROUPS = [(1, 0), (3, 2), (5, 4), (7, 6), (8, None)]
+CHUNKS = [(38, None, 0, 4), (38, (0, 1), 0, 2), (36, None, 0, 5), (36, (0, 1), 0, 3), (26, None, 0, 7),
+          (26, (0, 1), 0, 1), (20, None, 0, 0), (20, (1, 0), 0, 0), (16, None, 0, 7)]
+GROUPS = [(0, 1), (2, 3), (4, 5), (6, 7), (8, None)]
 NK = len(CHUNKS)
 MAXC = 12
 SCRATCH = {}
@@ -33,7 +33,7 @@ def rank_program(g, core, T, topo):
         return DstId(rid=rid, pnc=pid)
 
     def direct(k, half):
-        n, via, rpar, rcore = CHUNKS[k]
+        n, rel, rpar, rcore = CHUNKS[k]
         tr = []
         for e in range(8):
             j = (pair + half * 8 + e) % R
@@ -42,14 +42,17 @@ def rank_program(g, core, T, topo):
         return tr
 
     def handover(k, half):
-        via = CHUNKS[k][1]
-        return [RemoteDMATransfer(dst_ids=[dst(base + via)], dma_engine_mask=1 << (8 + e), remote_sem=hp[k],
-                                  src=xs[k][half * 8 + e], dst=xs[k][half * 8 + e]) for e in range(8)]
+        tr = []
+        for e in range(8):
+            j = (pair + half * 8 + e) % R
+            tr.append(RemoteDMATransfer(dst_ids=[dst(base + CHUNKS[k][1][half])], dma_engine_mask=1 << (8 + e),
+                                        remote_sem=hp[k], src=xs[k][j], dst=xs[k][j]))
+        return tr
 
     sent = 0
     if par == 0 and idx == 6:
         stq = [s.st0, s.st1]
-        qi = [0 if c[1] is None else 1 for c in CHUNKS]
+        qi = [1 if c[1] else 0 for c in CHUNKS]
         q = [g.sync, g.scalar]
         for k in range(NK):
             q[qi[k]].dma_start(xs[k][:], T.x[row0[k]:row0[k + 1], :]).then_inc(ld[k], 16)
@@ -77,13 +80,13 @@ def rank_program(g, core, T, topo):
         g.wait_ge(s.sent, sent)
         return
     for k in range(NK):
-        if par == 0 and CHUNKS[k][1] == idx:
-            g.wait_ge(hp[k], 16)
-            for half in range(2):
-                g.remote_dma_fused(direct(k, half), local_sem=s.sent)
-            sent += 16
+        rel = CHUNKS[k][1]
+        if par == 0 and rel and idx in rel:
+            g.wait_ge(hp[k], 8)
+            g.remote_dma_fused(direct(k, rel.index(idx)), local_sem=s.sent)
+            sent += 8
     for k in range(NK):
-        n, via, rpar, rcore = CHUNKS[k]
+        n, rel, rpar, rcore = CHUNKS[k]
         if par == rpar and idx == rcore:
             g.wait_ge(rs[k], 16)
             to = [(pair + t) % R for t in range(R)]

from concourse.bass import DstId, RemoteDMATransfer

R = 16
CHUNKS = [(38, None, 0, 4), (38, (0, 1), 0, 2), (36, None, 0, 5), (36, (0, 1), 0, 3), (26, None, 0, 7),
          (26, (0, 1), 0, 1), (20, None, 0, 0), (20, (1, 0), 0, 0), (16, None, 0, 7)]
GROUPS = [(0, 1), (2, 3), (4, 5), (6, 7), (8, None)]
NK = len(CHUNKS)
MAXC = 12
SCRATCH = {}
for k in range(MAXC):
    shape = [R, 128, CHUNKS[k][0]] if k < NK else [1, 128, 2]
    SCRATCH['xs%d' % k] = ('dram', shape, 'bfloat16')
    SCRATCH['ln%d' % k] = ('dram', shape, 'bfloat16')
SEMAPHORES = (['ld%d' % k for k in range(MAXC)] + ['hp%d' % k for k in range(MAXC)] + ['rs%d' % k for k in range(MAXC)]
              + ['ag%d' % k for k in range(MAXC)] + ['sent', 'st0', 'st1'])


def rank_program(g, core, T, topo):
    xs = [T.xs0, T.xs1, T.xs2, T.xs3, T.xs4, T.xs5, T.xs6, T.xs7, T.xs8, T.xs9, T.xs10, T.xs11]
    ln = [T.ln0, T.ln1, T.ln2, T.ln3, T.ln4, T.ln5, T.ln6, T.ln7, T.ln8, T.ln9, T.ln10, T.ln11]
    s = T.sem
    ld = [s.ld0, s.ld1, s.ld2, s.ld3, s.ld4, s.ld5, s.ld6, s.ld7, s.ld8, s.ld9, s.ld10, s.ld11]
    hp = [s.hp0, s.hp1, s.hp2, s.hp3, s.hp4, s.hp5, s.hp6, s.hp7, s.hp8, s.hp9, s.hp10, s.hp11]
    rs = [s.rs0, s.rs1, s.rs2, s.rs3, s.rs4, s.rs5, s.rs6, s.rs7, s.rs8, s.rs9, s.rs10, s.rs11]
    ag = [s.ag0, s.ag1, s.ag2, s.ag3, s.ag4, s.ag5, s.ag6, s.ag7, s.ag8, s.ag9, s.ag10, s.ag11]
    pair, within = (core // 16, core % 16)
    par, idx = (within // 8, within % 8)
    base = pair * 16
    row0 = [sum(c[0] for c in CHUNKS[:k]) // 2 for k in range(NK + 1)]

    def dst(d):
        rid, pid = topo.addr(d, core)
        return DstId(rid=rid, pnc=pid)

    def direct(k, half):
        n, rel, rpar, rcore = CHUNKS[k]
        tr = []
        for e in range(8):
            j = (pair + half * 8 + e) % R
            tr.append(RemoteDMATransfer(dst_ids=[dst(j * 16 + rpar * 8 + rcore)], dma_engine_mask=1 << e,
                                        remote_sem=rs[k], src=xs[k][j], dst=ln[k][pair]))
        return tr

    def handover(k, half):
        tr = []
        for e in range(8):
            j = (pair + half * 8 + e) % R
            tr.append(RemoteDMATransfer(dst_ids=[dst(base + CHUNKS[k][1][half])], dma_engine_mask=1 << (8 + e),
                                        remote_sem=hp[k], src=xs[k][j], dst=xs[k][j]))
        return tr

    sent = 0
    if par == 0 and idx == 6:
        stq = [s.st0, s.st1]
        qi = [1 if c[1] else 0 for c in CHUNKS]
        q = [g.sync, g.scalar]
        for k in range(NK):
            q[qi[k]].dma_start(xs[k][:], T.x[row0[k]:row0[k + 1], :]).then_inc(ld[k], 16)
        for kd, kr in GROUPS:
            if kr is not None:
                g.wait_ge(ld[kr], 16)
            if kd is not None:
                g.wait_ge(ld[kd], 16)
            for half in range(2):
                tr = []
                if kd is not None:
                    tr += direct(kd, half)
                if kr is not None:
                    tr += handover(kr, half)
                g.remote_dma_fused(tr, local_sem=s.sent)
                sent += len(tr)
        cnt = [0, 0]
        for k in range(NK):
            q[qi[k]].wait_ge(ag[k], 8 * R)
            q[qi[k]].dma_start(T.y[row0[k]:row0[k + 1], :], ln[k][:]).then_inc(stq[qi[k]], 16)
            cnt[qi[k]] += 16
        for i in range(2):
            if cnt[i]:
                q[i].wait_ge(stq[i], cnt[i])
        g.wait_ge(s.sent, sent)
        return
    for k in range(NK):
        rel = CHUNKS[k][1]
        if par == 0 and rel and idx in rel:
            g.wait_ge(hp[k], 8)
            g.remote_dma_fused(direct(k, rel.index(idx)), local_sem=s.sent)
            sent += 8
    for k in range(NK):
        n, rel, rpar, rcore = CHUNKS[k]
        if par == rpar and idx == rcore:
            g.wait_ge(rs[k], 16)
            to = [(pair + t) % R for t in range(R)]
            g.remote_dma_fused([RemoteDMATransfer(dst_ids=[dst(i * 16 + 6) for i in to], dma_engine_mask=255,
                                                  remote_sem=ag[k], srcs=[ln[k][r] for r in range(R)],
                                                  dsts=[ln[k][pair] for i in to], alu_op=1)], local_sem=s.sent)
            sent += 8
    if sent:
        g.wait_ge(s.sent, sent)
